import numpy as np, ml_dtypes
CORES = [8,136,40,168]
N = 4
import mx_ref
NC, G = 256, 2
C = np.float32(0.047)
BF = ml_dtypes.bfloat16
def cut(t, i, w=512):
    return t[:, w * i:w * i + w]
def tile(rs):
    return np.stack(rs, axis=2).reshape(128, -1).astype(BF)
def layer(w, X):
    out = []
    for i in range(G):
        for t in range(len(X)):
            p = mx_ref.matmul(mx_ref.quantize(cut(w, len(X) * i + t)), X[t])
            z = p if t == 0 else z + p
        out.append(z)
    return out
def act(Z):
    return [np.maximum(s * z, 0) * C for z in Z for s in (1, -1)]
def turned(R):
    return [np.concatenate([R[b][:, 128 * t:128 * t + 128].T for b in range(4)], axis=1) for t in range(4)]
def setup_inputs(rng):
    def f(*shape):
        return mx_ref.flush((rng.standard_normal(shape, dtype=np.float32) * np.exp2(rng.integers(-2, 3, shape[:-1] + (1,)))).astype(BF))
    return {"x": f(N, 128, 4 * 512), "w1": f(N, 128, G * 512), "w2": f(N, 128, 512), "e": f(N, 128, 4 * NC)}
def setup_inputs_blocks(rng):
    d = setup_inputs(rng)
    for k in ("x", "w1", "w2", "e"): d[k] = mx_ref.spread(d[k], rng, 4)
    return d
def setup_inputs_wide(rng):
    d = setup_inputs(rng)
    for k in ("x", "w1", "w2", "e"): d[k] = mx_ref.flush((d[k].astype(np.float32) * np.exp2(rng.integers(-6, 7, (N, 1, 1))).astype(np.float32)).astype(BF))
    return d
def setup_inputs_zeros(rng):
    d = setup_inputs(rng); v = d["x"].reshape(N, 128, -1, 4).copy()
    v[np.broadcast_to((rng.random((N, 1, v.shape[2], 1)) < 0.33), v.shape)] = 0
    d["x"] = v.reshape(d["x"].shape)
    return d
def reference(x, w1, w2, e):
    R = [act(layer(w1[j], [mx_ref.quantize(x[j])])) for j in range(N)]
    H = [mx_ref.quantize(tile(R[j])) for j in range(N)]
    K = [tile(turned(R[j])) for j in range(N)]
    y = np.zeros((N, 128, 512), np.float32); z = np.zeros((N, 128, 4 * NC), np.float32)
    for r in range(N):
        y[r] = mx_ref.matmul(mx_ref.quantize(w2[r]), H[(r - 1) % N]); qe = mx_ref.quantize(e[r])
        for b in range(4):
            z[r][:, NC * b:NC * b + NC] = mx_ref.matmul(mx_ref.quantize(cut(K[(r + 1) % N], b)), qe)
    return {"y": y, "z": z}

@@ -1,0 +1,138 @@
+import numpy as np
+from concourse.mybir import dt, AluOpType, ActivationFunctionType
+
+CODE, PLANE, BF16, F32 = "float8_e4m3fn_x4", "uint8", "bfloat16", "float32"
+C = float(np.float32(0.047))
+ORDER = [0, 2, 1, 3]
+
+SCRATCH = {
+    "xs": ("sbuf", [128, 2048], BF16), "w1s": ("sbuf", [128, 1024], BF16),
+    "w2s": ("sbuf", [128, 512], BF16), "es": ("sbuf", [128, 1024], BF16),
+    "xq": ("sbuf", [128, 512], CODE), "xp": ("sbuf", [128, 512], PLANE),
+    "w1q": ("sbuf", [128, 256], CODE), "w1p": ("sbuf", [128, 256], PLANE),
+    "w2q": ("sbuf", [128, 128], CODE), "w2p": ("sbuf", [128, 128], PLANE),
+    "eq": ("sbuf", [128, 256], CODE), "ep": ("sbuf", [128, 256], PLANE),
+    "ht": ("sbuf", [128, 2048], BF16), "kt": ("sbuf", [128, 2048], BF16),
+    "hq": ("sbuf", [128, 512], CODE), "hp": ("sbuf", [128, 512], PLANE),
+    "kq": ("sbuf", [128, 512], CODE), "kp": ("sbuf", [128, 512], PLANE),
+    "rhq": ("sbuf", [128, 512], CODE), "rhp": ("sbuf", [128, 512], PLANE),
+    "rkq": ("sbuf", [128, 512], CODE), "rkp": ("sbuf", [128, 512], PLANE),
+    "yo": ("sbuf", [128, 512], F32), "zo": ("sbuf", [128, 1024], F32),
+    "pk": ("psum", [128, 2048], F32), "pz": ("psum", [128, 1024], F32), "py": ("psum", [128, 1024], F32),
+}
+SEMAPHORES = (["lx0", "lx1", "lw1", "lw2", "le", "qw1", "qx0", "qx1", "qk", "qh", "qe", "qw2", "aks", "akv", "ahs", "ahv",
+               "rk", "rh", "sent", "sty", "stz"]
+              + ["mk%d" % t for t in range(4)] + ["mh%d" % i for i in range(2)]
+              + ["mz%d" % b for b in range(4)] + ["ez%d" % b for b in range(4)]
+              + ["my%d" % i for i in range(2)] + ["ey%d" % i for i in range(2)])
+
+
+def engines(topo, src, dst):
+    return bin(topo.mask(src, dst)).count("1")
+
+
+def rank_program(g, core, T, topo):
+    rank = T.rank_of(core)
+    if rank is None:
+        return
+    n = len(T.cores)
+    S = T.sem
+    te, ve, se, sy = g.tensor, g.vector, g.scalar, g.sync
+    relu, copy = ActivationFunctionType.Relu, ActivationFunctionType.Copy
+    before, behind = T.cores[(rank - 1) % n], T.cores[(rank + 1) % n]
+
+    def part(q, out, src, sign):
+        if q is se:
+            return se.activation(out, src, relu, scale=sign * C)
+        return ve.tensor_scalar(out, src, sign * C, 0.0, AluOpType.mult, AluOpType.max)
+
+    se.dma_start(T.w1s[:], T.w1[:]).then_inc(S.lw1, 16)
+    sy.dma_start(T.xs[:, 0:1024], T.x[:, 0:1024]).then_inc(S.lx0, 16)
+    sy.dma_start(T.xs[:, 1024:2048], T.x[:, 1024:2048]).then_inc(S.lx1, 16)
+    sy.wait_ge(S.lx0, 16)
+    sy.dma_start(T.es[:], T.e[:]).then_inc(S.le, 16)
+    sy.dma_start(T.w2s[:], T.w2[:]).then_inc(S.lw2, 16)
+
+    te.wait_ge(S.qw1, 1)
+    for t in range(4):
+        if t % 2 == 0:
+            te.wait_ge(S["qx%d" % (t // 2)], 1)
+        te.matmul_mx(T.pk[:, 512 * t:512 * t + 256], T.xq[:, 128 * t:128 * t + 128], T.xp[:, 128 * t:128 * t + 128],
+                     T.w1q[:, 0:256], T.w1p[:, 0:256], True, True).then_inc(S["mk%d" % t], 1)
+    for i in range(2):
+        te.matmul_mx(T.pz[:, 512 * i:512 * i + 512], T.w1q[:, 128 * i:128 * i + 128], T.w1p[:, 128 * i:128 * i + 128],
+                     T.xq[:, 0:512], T.xp[:, 0:512], True, True).then_inc(S["mh%d" % i], 1)
+    te.wait_ge(S.qe, 1)
+    te.wait_ge(S.aks, 6)
+    te.wait_ge(S.akv, 2)
+    te.wait_ge(S.rk, 2 * engines(topo, behind, core))
+    for b in range(4):
+        c = 128 * ORDER.index(b)
+        te.matmul_mx(T.pk[:, 512 * b:512 * b + 256], T.rkq[:, c:c + 128], T.rkp[:, c:c + 128],
+                     T.eq[:, 0:256], T.ep[:, 0:256], True, True).then_inc(S["mz%d" % b], 1)
+    te.wait_ge(S.qw2, 1)
+    te.wait_ge(S.rh, 2 * engines(topo, before, core))
+    for i in range(2):
+        te.matmul_mx(T.py[:, 512 * i:512 * i + 256], T.w2q[:, 0:128], T.w2p[:, 0:128],
+                     T.rhq[:, 256 * i:256 * i + 256], T.rhp[:, 256 * i:256 * i + 256], True, True).then_inc(S["my%d" % i], 1)
+
+    for t in range(3):
+        se.wait_ge(S["mk%d" % t], 1)
+        for half, sign in ((0, 1.0), (1, -1.0)):
+            part(se, T.kt[:, 1024 * half + t:1024 * half + 1024:4], T.pk[:, 512 * t:512 * t + 256], sign).then_inc(S.aks, 1)
+    se.wait_ge(S.mh0, 1)
+    for b, sign in ((0, 1.0), (1, -1.0)):
+        part(se, T.ht[:, b:2048:4], T.pz[:, 0:512], sign).then_inc(S.ahs, 1)
+    for b in (0, 2):
+        se.wait_ge(S["mz%d" % b], 1)
+        se.activation(T.zo[:, 256 * b:256 * b + 256], T.pk[:, 512 * b:512 * b + 256], copy).then_inc(S["ez%d" % b], 1)
+    se.wait_ge(S.my0, 1)
+    se.activation(T.yo[:, 0:256], T.py[:, 0:256], copy).then_inc(S.ey0, 1)
+    se.wait_ge(S.ey0, 1)
+    se.dma_start(T.y[:, 0:256], T.yo[:, 0:256]).then_inc(S.sty, 16)
+
+    ve.wait_ge(S.lw1, 16)
+    ve.quantize_mx(T.w1q[:, 0:256], T.w1p[:, 0:256], T.w1s[:, 0:1024]).then_inc(S.qw1, 1)
+    for i in range(2):
+        ve.wait_ge(S["lx%d" % i], 16)
+        ve.quantize_mx(T.xq[:, 256 * i:256 * i + 256], T.xp[:, 256 * i:256 * i + 256],
+                       T.xs[:, 1024 * i:1024 * i + 1024]).then_inc(S["qx%d" % i], 1)
+    ve.wait_ge(S.mk3, 1)
+    for half, sign in ((0, 1.0), (1, -1.0)):
+        part(ve, T.kt[:, 1024 * half + 3:1024 * half + 1024:4], T.pk[:, 1536:1792], sign).then_inc(S.akv, 1)
+    ve.wait_ge(S.akv, 2)
+    ve.wait_ge(S.aks, 6)
+    ve.quantize_mx(T.kq[:, 0:512], T.kp[:, 0:512], T.kt[:, 0:2048]).then_inc(S.qk, 1)
+    ve.wait_ge(S.mh1, 1)
+    for b, sign in ((2, 1.0), (3, -1.0)):
+        part(ve, T.ht[:, b:2048:4], T.pz[:, 512:1024], sign).then_inc(S.ahv, 1)
+    ve.wait_ge(S.ahv, 2)
+    ve.wait_ge(S.ahs, 2)
+    ve.quantize_mx(T.hq[:, 0:512], T.hp[:, 0:512], T.ht[:, 0:2048]).then_inc(S.qh, 1)
+    ve.wait_ge(S.le, 16)
+    ve.quantize_mx(T.eq[:, 0:256], T.ep[:, 0:256], T.es[:, 0:1024]).then_inc(S.qe, 1)
+    ve.wait_ge(S.lw2, 16)
+    ve.quantize_mx(T.w2q[:, 0:128], T.w2p[:, 0:128], T.w2s[:, 0:512]).then_inc(S.qw2, 1)
+    for b in (1, 3):
+        ve.wait_ge(S["mz%d" % b], 1)
+        ve.tensor_copy(T.zo[:, 256 * b:256 * b + 256], T.pk[:, 512 * b:512 * b + 256]).then_inc(S["ez%d" % b], 1)
+    ve.wait_ge(S.my1, 1)
+    ve.tensor_copy(T.yo[:, 256:512], T.py[:, 512:768]).then_inc(S.ey1, 1)
+
+    for q, dst, codes, land_c, plane, land_p, arrive in ((S.qk, before, T.kq, T.rkq, T.kp, T.rkp, S.rk),
+                                                         (S.qh, behind, T.hq, T.rhq, T.hp, T.rhp, S.rh)):
+        rid, pid = topo.addr(dst, core)
+        m = topo.mask(core, dst)
+        g.wait_ge(q, 1)
+        g.remote_dma(land_c[:, 0:512].bitcast(dt.uint8), codes[:, 0:512].bitcast(dt.uint8), arrive, S.sent, pid, rid, m)
+        g.remote_dma(land_p[:, 0:512], plane[:, 0:512], arrive, S.sent, pid, rid, m)
+    g.wait_ge(S.sent, 2 * (engines(topo, core, before) + engines(topo, core, behind)))
+
+    for b in range(4):
+        sy.wait_ge(S["ez%d" % b], 1)
+        if b % 2:
+            sy.dma_start(T.z[:, 256 * b - 256:256 * b + 256], T.zo[:, 256 * b - 256:256 * b + 256]).then_inc(S.stz, 16)
+    sy.wait_ge(S.ey1, 1)
+    sy.dma_start(T.y[:, 256:512], T.yo[:, 256:512]).then_inc(S.sty, 16)
+    sy.wait_ge(S.stz, 32)
+    sy.wait_ge(S.sty, 32)

@@ -18,13 +18,14 @@ SCRATCH = {
     "rhq": ("sbuf", [128, 512], CODE), "rhp": ("sbuf", [128, 512], PLANE),
     "rkq": ("sbuf", [128, 512], CODE), "rkp": ("sbuf", [128, 512], PLANE),
     "yo": ("sbuf", [128, 512], F32), "zo": ("sbuf", [128, 1024], F32),
-    "pk": ("psum", [128, 2048], F32), "pz": ("psum", [128, 1024], F32), "py": ("psum", [128, 1024], F32),
+    "pk": ("psum", [128, 2048], F32), "pz": ("psum", [128, 2048], F32),
 }
-SEMAPHORES = (["lx0", "lx1", "lw1", "lw2", "le", "qw1", "qx0", "qx1", "qk", "qh", "qe", "qw2", "aks", "akv", "ahs", "ahv",
-               "rk", "rh", "sent", "sty", "stz"]
-              + ["mk%d" % t for t in range(4)] + ["mh%d" % i for i in range(2)]
+SEMAPHORES = (["lx0", "lx1", "lw1", "lw2", "le", "qw1", "qx0", "qx1", "qk", "qh0", "qh1", "qe", "qw2", "aks", "akv",
+               "ahs0", "ahs1", "ahv0", "ahv1", "rk", "rh0", "rh1", "rhp", "sent", "stys", "stya", "stz"]
+              + ["mk%d" % t for t in range(4)] + ["mh%d" % i for i in range(4)]
               + ["mz%d" % b for b in range(4)] + ["ez%d" % b for b in range(4)]
-              + ["my%d" % i for i in range(2)] + ["ey%d" % i for i in range(2)])
+              + ["my%d" % i for i in range(3)] + ["ey%d" % i for i in range(3)])
+YCUT = ((0, 256), (256, 128), (384, 128))
 
 
 def engines(topo, src, dst):
@@ -40,11 +41,23 @@ def rank_program(g, core, T, topo):
     te, ve, se, sy = g.tensor, g.vector, g.scalar, g.sync
     relu, copy = ActivationFunctionType.Relu, ActivationFunctionType.Copy
     before, behind = T.cores[(rank - 1) % n], T.cores[(rank + 1) % n]
+    signs = ((0, 1.0), (1, -1.0))
 
     def part(q, out, src, sign):
         if q is se:
             return se.activation(out, src, relu, scale=sign * C)
         return ve.tensor_scalar(out, src, sign * C, 0.0, AluOpType.mult, AluOpType.max)
+
+    def k_parts(q, t, sem):
+        q.wait_ge(S["mk%d" % t], 1)
+        for s, sign in signs:
+            part(q, T.kt[:, 1024 * s + t:1024 * s + 1024:4], T.pk[:, 512 * t:512 * t + 256], sign).then_inc(sem, 1)
+
+    def h_parts(q, half, i, sem):
+        q.wait_ge(S["mh%d" % (2 * half + i)], 1)
+        for s, sign in signs:
+            part(q, T.ht[:, 1024 * half + 2 * i + s:1024 * half + 1024:4],
+                 T.pz[:, 1024 * half + 512 * i:1024 * half + 512 * i + 256], sign).then_inc(sem, 1)
 
     se.dma_start(T.w1s[:], T.w1[:]).then_inc(S.lw1, 16)
     sy.dma_start(T.xs[:, 0:1024], T.x[:, 0:1024]).then_inc(S.lx0, 16)
@@ -53,15 +66,26 @@ def rank_program(g, core, T, topo):
     sy.dma_start(T.es[:], T.e[:]).then_inc(S.le, 16)
     sy.dma_start(T.w2s[:], T.w2[:]).then_inc(S.lw2, 16)
 
-    te.wait_ge(S.qw1, 1)
-    for t in range(4):
-        if t % 2 == 0:
-            te.wait_ge(S["qx%d" % (t // 2)], 1)
+    def plain(half):
+        for i in range(2):
+            b = 1024 * half + 512 * i
+            te.matmul_mx(T.pz[:, b:b + 256], T.w1q[:, 128 * i:128 * i + 128], T.w1p[:, 128 * i:128 * i + 128],
+                         T.xq[:, 256 * half:256 * half + 256], T.xp[:, 256 * half:256 * half + 256],
+                         True, True).then_inc(S["mh%d" % (2 * half + i)], 1)
+
+    def turned(t):
         te.matmul_mx(T.pk[:, 512 * t:512 * t + 256], T.xq[:, 128 * t:128 * t + 128], T.xp[:, 128 * t:128 * t + 128],
                      T.w1q[:, 0:256], T.w1p[:, 0:256], True, True).then_inc(S["mk%d" % t], 1)
-    for i in range(2):
-        te.matmul_mx(T.pz[:, 512 * i:512 * i + 512], T.w1q[:, 128 * i:128 * i + 128], T.w1p[:, 128 * i:128 * i + 128],
-                     T.xq[:, 0:512], T.xp[:, 0:512], True, True).then_inc(S["mh%d" % i], 1)
+
+    te.wait_ge(S.qw1, 1)
+    te.wait_ge(S.qx0, 1)
+    plain(0)
+    turned(0)
+    turned(1)
+    te.wait_ge(S.qx1, 1)
+    turned(2)
+    turned(3)
+    plain(1)
     te.wait_ge(S.qe, 1)
     te.wait_ge(S.aks, 6)
     te.wait_ge(S.akv, 2)
@@ -71,68 +95,89 @@ def rank_program(g, core, T, topo):
         te.matmul_mx(T.pk[:, 512 * b:512 * b + 256], T.rkq[:, c:c + 128], T.rkp[:, c:c + 128],
                      T.eq[:, 0:256], T.ep[:, 0:256], True, True).then_inc(S["mz%d" % b], 1)
     te.wait_ge(S.qw2, 1)
-    te.wait_ge(S.rh, 2 * engines(topo, before, core))
-    for i in range(2):
-        te.matmul_mx(T.py[:, 512 * i:512 * i + 256], T.w2q[:, 0:128], T.w2p[:, 0:128],
-                     T.rhq[:, 256 * i:256 * i + 256], T.rhp[:, 256 * i:256 * i + 256], True, True).then_inc(S["my%d" % i], 1)
+    for s in ("ahs0", "ahv0", "ahs1", "ahv1"):
+        te.wait_ge(S[s], 2)
+    for s in ("rh0", "rhp"):
+        te.wait_ge(S[s], engines(topo, before, core))
+    for i, (c, w) in enumerate(YCUT):
+        if i == 1:
+            te.wait_ge(S.rh1, engines(topo, before, core))
+        te.matmul_mx(T.pz[:, 512 * i:512 * i + w], T.w2q[:, 0:128], T.w2p[:, 0:128],
+                     T.rhq[:, c:c + w], T.rhp[:, c:c + w], True, True).then_inc(S["my%d" % i], 1)
 
+    def z_out(q, b):
+        q.wait_ge(S["mz%d" % b], 1)
+        o, i = T.zo[:, 256 * b:256 * b + 256], T.pk[:, 512 * b:512 * b + 256]
+        (se.activation(o, i, copy) if q is se else ve.tensor_copy(o, i)).then_inc(S["ez%d" % b], 1)
+
+    def y_out(q, j):
+        c, w = YCUT[j]
+        q.wait_ge(S["my%d" % j], 1)
+        o, i = T.yo[:, c:c + w], T.pz[:, 512 * j:512 * j + w]
+        (se.activation(o, i, copy) if q is se else ve.tensor_copy(o, i)).then_inc(S["ey%d" % j], 1)
+
+    h_parts(se, 0, 0, S.ahs0)
     for t in range(3):
-        se.wait_ge(S["mk%d" % t], 1)
-        for half, sign in ((0, 1.0), (1, -1.0)):
-            part(se, T.kt[:, 1024 * half + t:1024 * half + 1024:4], T.pk[:, 512 * t:512 * t + 256], sign).then_inc(S.aks, 1)
-    se.wait_ge(S.mh0, 1)
-    for b, sign in ((0, 1.0), (1, -1.0)):
-        part(se, T.ht[:, b:2048:4], T.pz[:, 0:512], sign).then_inc(S.ahs, 1)
-    for b in (0, 2):
-        se.wait_ge(S["mz%d" % b], 1)
-        se.activation(T.zo[:, 256 * b:256 * b + 256], T.pk[:, 512 * b:512 * b + 256], copy).then_inc(S["ez%d" % b], 1)
-    se.wait_ge(S.my0, 1)
-    se.activation(T.yo[:, 0:256], T.py[:, 0:256], copy).then_inc(S.ey0, 1)
-    se.wait_ge(S.ey0, 1)
-    se.dma_start(T.y[:, 0:256], T.yo[:, 0:256]).then_inc(S.sty, 16)
+        k_parts(se, t, S.aks)
+    h_parts(se, 1, 0, S.ahs1)
+    z_out(se, 0)
+    z_out(se, 2)
+    y_out(se, 0)
+    y_out(se, 1)
+    se.wait_ge(S.ey1, 1)
+    se.wait_ge(S.ey2, 1)
+    se.dma_start(T.y[:, 256:512], T.yo[:, 256:512]).then_inc(S.stya, 16)
+    se.wait_ge(S.stya, 16)
 
     ve.wait_ge(S.lw1, 16)
     ve.quantize_mx(T.w1q[:, 0:256], T.w1p[:, 0:256], T.w1s[:, 0:1024]).then_inc(S.qw1, 1)
-    for i in range(2):
-        ve.wait_ge(S["lx%d" % i], 16)
-        ve.quantize_mx(T.xq[:, 256 * i:256 * i + 256], T.xp[:, 256 * i:256 * i + 256],
-                       T.xs[:, 1024 * i:1024 * i + 1024]).then_inc(S["qx%d" % i], 1)
-    ve.wait_ge(S.mk3, 1)
-    for half, sign in ((0, 1.0), (1, -1.0)):
-        part(ve, T.kt[:, 1024 * half + 3:1024 * half + 1024:4], T.pk[:, 1536:1792], sign).then_inc(S.akv, 1)
+    ve.wait_ge(S.lx0, 16)
+    ve.quantize_mx(T.xq[:, 0:256], T.xp[:, 0:256], T.xs[:, 0:1024]).then_inc(S.qx0, 1)
+    h_parts(ve, 0, 1, S.ahv0)
+    ve.wait_ge(S.lx1, 16)
+    ve.quantize_mx(T.xq[:, 256:512], T.xp[:, 256:512], T.xs[:, 1024:2048]).then_inc(S.qx1, 1)
+    ve.wait_ge(S.ahv0, 2)
+    ve.wait_ge(S.ahs0, 2)
+    ve.quantize_mx(T.hq[:, 0:256], T.hp[:, 0:256], T.ht[:, 0:1024]).then_inc(S.qh0, 1)
+    k_parts(ve, 3, S.akv)
     ve.wait_ge(S.akv, 2)
     ve.wait_ge(S.aks, 6)
     ve.quantize_mx(T.kq[:, 0:512], T.kp[:, 0:512], T.kt[:, 0:2048]).then_inc(S.qk, 1)
-    ve.wait_ge(S.mh1, 1)
-    for b, sign in ((2, 1.0), (3, -1.0)):
-        part(ve, T.ht[:, b:2048:4], T.pz[:, 512:1024], sign).then_inc(S.ahv, 1)
-    ve.wait_ge(S.ahv, 2)
-    ve.wait_ge(S.ahs, 2)
-    ve.quantize_mx(T.hq[:, 0:512], T.hp[:, 0:512], T.ht[:, 0:2048]).then_inc(S.qh, 1)
+    h_parts(ve, 1, 1, S.ahv1)
+    ve.wait_ge(S.ahv1, 2)
+    ve.wait_ge(S.ahs1, 2)
+    ve.quantize_mx(T.hq[:, 256:512], T.hp[:, 256:512], T.ht[:, 1024:2048]).then_inc(S.qh1, 1)
     ve.wait_ge(S.le, 16)
     ve.quantize_mx(T.eq[:, 0:256], T.ep[:, 0:256], T.es[:, 0:1024]).then_inc(S.qe, 1)
     ve.wait_ge(S.lw2, 16)
     ve.quantize_mx(T.w2q[:, 0:128], T.w2p[:, 0:128], T.w2s[:, 0:512]).then_inc(S.qw2, 1)
-    for b in (1, 3):
-        ve.wait_ge(S["mz%d" % b], 1)
-        ve.tensor_copy(T.zo[:, 256 * b:256 * b + 256], T.pk[:, 512 * b:512 * b + 256]).then_inc(S["ez%d" % b], 1)
-    ve.wait_ge(S.my1, 1)
-    ve.tensor_copy(T.yo[:, 256:512], T.py[:, 512:768]).then_inc(S.ey1, 1)
+    z_out(ve, 1)
+    z_out(ve, 3)
+    y_out(ve, 2)
 
-    for q, dst, codes, land_c, plane, land_p, arrive in ((S.qk, before, T.kq, T.rkq, T.kp, T.rkp, S.rk),
-                                                         (S.qh, behind, T.hq, T.rhq, T.hp, T.rhp, S.rh)):
+    def codes(dst, land, src, a, b, arrive):
         rid, pid = topo.addr(dst, core)
-        m = topo.mask(core, dst)
-        g.wait_ge(q, 1)
-        g.remote_dma(land_c[:, 0:512].bitcast(dt.uint8), codes[:, 0:512].bitcast(dt.uint8), arrive, S.sent, pid, rid, m)
-        g.remote_dma(land_p[:, 0:512], plane[:, 0:512], arrive, S.sent, pid, rid, m)
-    g.wait_ge(S.sent, 2 * (engines(topo, core, before) + engines(topo, core, behind)))
+        g.remote_dma(land[:, a:b].bitcast(dt.uint8), src[:, a:b].bitcast(dt.uint8), arrive, S.sent, pid, rid, topo.mask(core, dst))
+
+    def plane(dst, land, src, arrive):
+        rid, pid = topo.addr(dst, core)
+        g.remote_dma(land[:, 0:512], src[:, 0:512], arrive, S.sent, pid, rid, topo.mask(core, dst))
+
+    g.wait_ge(S.qh0, 1)
+    codes(behind, T.rhq, T.hq, 0, 256, S.rh0)
+    g.wait_ge(S.qk, 1)
+    codes(before, T.rkq, T.kq, 0, 512, S.rk)
+    plane(before, T.rkp, T.kp, S.rk)
+    g.wait_ge(S.qh1, 1)
+    plane(behind, T.rhp, T.hp, S.rhp)
+    codes(behind, T.rhq, T.hq, 256, 512, S.rh1)
+    g.wait_ge(S.sent, 3 * engines(topo, core, behind) + 2 * engines(topo, core, before))
 
     for b in range(4):
         sy.wait_ge(S["ez%d" % b], 1)
         if b % 2:
             sy.dma_start(T.z[:, 256 * b - 256:256 * b + 256], T.zo[:, 256 * b - 256:256 * b + 256]).then_inc(S.stz, 16)
-    sy.wait_ge(S.ey1, 1)
-    sy.dma_start(T.y[:, 256:512], T.yo[:, 256:512]).then_inc(S.sty, 16)
+    sy.wait_ge(S.ey0, 1)
+    sy.dma_start(T.y[:, 0:256], T.yo[:, 0:256]).then_inc(S.stys, 16)
     sy.wait_ge(S.stz, 32)
-    sy.wait_ge(S.sty, 32)
+    sy.wait_ge(S.stys, 16)

@@ -4,6 +4,16 @@ from concourse.mybir import dt, AluOpType, ActivationFunctionType
 CODE, PLANE, BF16, F32 = "float8_e4m3fn_x4", "uint8", "bfloat16", "float32"
 C = float(np.float32(0.047))
 ORDER = [0, 2, 1, 3]
+XL = ((0, 128), (128, 512))
+XQ = ((0, 128), (128, 256), (256, 512))
+HP = ((0, 128), (128, 256), (256, 512))
+KP = ((0, 256), (256, 512))
+YP = ((0, 256), (256, 384), (384, 512))
+YS = (((0, 256), (0,)), ((256, 512), (1, 2)))
+TENSOR = "h0 k0 h1 k1 k2 k3 h2".split()
+SCALAR = "h000 h001 k00 k01 h100 h101 k10 k20 k11 k21 h200 h201 z0 z1 y0 y1".split()
+VECTOR = "w1 x0 h010 h011 x1 H0 x2 h110 h111 H1 k30 K0 k31 K1 h210 h211 H2 e w2 z2 z3 y2".split()
+SENDS = "h0 h1 k0 kp k1 hp h2".split()
 
 SCRATCH = {
     "xs": ("sbuf", [128, 2048], BF16), "w1s": ("sbuf", [128, 1024], BF16),
@@ -20,16 +30,20 @@ SCRATCH = {
     "yo": ("sbuf", [128, 512], F32), "zo": ("sbuf", [128, 1024], F32),
     "pk": ("psum", [128, 2048], F32), "pz": ("psum", [128, 2048], F32),
 }
-SEMAPHORES = (["lx0", "lx1", "lw1", "lw2", "le", "qw1", "qx0", "qx1", "qk", "qh0", "qh1", "qe", "qw2", "aks", "akv",
-               "ahs0", "ahs1", "ahv0", "ahv1", "rk", "rh0", "rh1", "rhp", "sent", "stys", "stya", "stz"]
-              + ["mk%d" % t for t in range(4)] + ["mh%d" % i for i in range(4)]
-              + ["mz%d" % b for b in range(4)] + ["ez%d" % b for b in range(4)]
-              + ["my%d" % i for i in range(3)] + ["ey%d" % i for i in range(3)])
-YCUT = ((0, 256), (256, 128), (384, 128))
+SEMAPHORES = (["lw1", "lw2", "le", "rkp", "rhp", "sent", "stz"] + ["lx%d" % i for i in range(len(XL))]
+              + ["rh%d" % i for i in range(len(HP))] + ["rk%d" % i for i in range(len(KP))]
+              + ["sty%d" % i for i in range(len(YS))]
+              + ["mk%d" % t for t in range(4)] + ["mh%d%d" % (p, i) for p in range(len(HP)) for i in range(2)]
+              + ["mz%d" % b for b in range(4)] + ["my%d" % j for j in range(len(YP))]
+              + ["a" + s for s in SCALAR] + ["a" + s for s in VECTOR])
 
 
 def engines(topo, src, dst):
     return bin(topo.mask(src, dst)).count("1")
+
+
+def over(pieces, a, b):
+    return [i for i, (c, d) in enumerate(pieces) if c < b and a < d]
 
 
 def rank_program(g, core, T, topo):
@@ -41,143 +55,142 @@ def rank_program(g, core, T, topo):
     te, ve, se, sy = g.tensor, g.vector, g.scalar, g.sync
     relu, copy = ActivationFunctionType.Relu, ActivationFunctionType.Copy
     before, behind = T.cores[(rank - 1) % n], T.cores[(rank + 1) % n]
-    signs = ((0, 1.0), (1, -1.0))
+    signs = (1.0, -1.0)
+
+    def need(q, *names):
+        for s in names:
+            q.wait_ge(S[s], 1)
+
+    def h_acts(p):
+        return ["ah%d%d%d" % (p, i, s) for i in range(2) for s in range(2)]
+
+    se.dma_start(T.w1s[:], T.w1[:]).then_inc(S.lw1, 16)
+    for i, (a, b) in enumerate(XL):
+        sy.dma_start(T.xs[:, 4 * a:4 * b], T.x[:, 4 * a:4 * b]).then_inc(S["lx%d" % i], 16)
+    sy.wait_ge(S.lx0, 16)
+    sy.dma_start(T.es[:], T.e[:]).then_inc(S.le, 16)
+    sy.dma_start(T.w2s[:], T.w2[:]).then_inc(S.lw2, 16)
+
+    need(te, "aw1")
+    for step in TENSOR:
+        j = int(step[1])
+        if step[0] == "h":
+            a, b = HP[j]
+            need(te, *["ax%d" % i for i in over(XQ, a, b)])
+            if j > 1:
+                need(te, *h_acts(j - 2))
+            for i in range(2):
+                c = 512 * ((2 * j + i) % 4)
+                te.matmul_mx(T.pz[:, c:c + b - a], T.w1q[:, 128 * i:128 * i + 128], T.w1p[:, 128 * i:128 * i + 128],
+                             T.xq[:, a:b], T.xp[:, a:b], True, True).then_inc(S["mh%d%d" % (j, i)], 1)
+        else:
+            a, b = 128 * j, 128 * j + 128
+            need(te, *["ax%d" % i for i in over(XQ, a, b)])
+            te.matmul_mx(T.pk[:, 512 * j:512 * j + 256], T.xq[:, a:b], T.xp[:, a:b],
+                         T.w1q[:, 0:256], T.w1p[:, 0:256], True, True).then_inc(S["mk%d" % j], 1)
+    need(te, "ae", *["ak%d%d" % (t, s) for t in range(4) for s in range(2)])
+    te.wait_ge(S.rkp, engines(topo, behind, core))
+    for b in ORDER:
+        c = 128 * ORDER.index(b)
+        for i in over(KP, c, c + 128):
+            te.wait_ge(S["rk%d" % i], engines(topo, behind, core))
+        te.matmul_mx(T.pk[:, 512 * b:512 * b + 256], T.rkq[:, c:c + 128], T.rkp[:, c:c + 128],
+                     T.eq[:, 0:256], T.ep[:, 0:256], True, True).then_inc(S["mz%d" % b], 1)
+    need(te, "aw2", *[s for p in range(len(HP)) for s in h_acts(p)])
+    te.wait_ge(S.rhp, engines(topo, before, core))
+    for j, (a, b) in enumerate(YP):
+        for i in over(HP, a, b):
+            te.wait_ge(S["rh%d" % i], engines(topo, before, core))
+        te.matmul_mx(T.pz[:, 512 * j:512 * j + b - a], T.w2q[:, 0:128], T.w2p[:, 0:128],
+                     T.rhq[:, a:b], T.rhp[:, a:b], True, True).then_inc(S["my%d" % j], 1)
 
     def part(q, out, src, sign):
         if q is se:
             return se.activation(out, src, relu, scale=sign * C)
         return ve.tensor_scalar(out, src, sign * C, 0.0, AluOpType.mult, AluOpType.max)
 
-    def k_parts(q, t, sem):
-        q.wait_ge(S["mk%d" % t], 1)
-        for s, sign in signs:
-            part(q, T.kt[:, 1024 * s + t:1024 * s + 1024:4], T.pk[:, 512 * t:512 * t + 256], sign).then_inc(sem, 1)
+    def out_of(q, out, src):
+        return se.activation(out, src, copy) if q is se else ve.tensor_copy(out, src)
 
-    def h_parts(q, half, i, sem):
-        q.wait_ge(S["mh%d" % (2 * half + i)], 1)
-        for s, sign in signs:
-            part(q, T.ht[:, 1024 * half + 2 * i + s:1024 * half + 1024:4],
-                 T.pz[:, 1024 * half + 512 * i:1024 * half + 512 * i + 256], sign).then_inc(sem, 1)
+    def turn(q, mine, step):
+        first = step[:-1] + "0"
+        if step[-1] == "1" and first not in mine:
+            need(q, "a" + first)
 
-    se.dma_start(T.w1s[:], T.w1[:]).then_inc(S.lw1, 16)
-    sy.dma_start(T.xs[:, 0:1024], T.x[:, 0:1024]).then_inc(S.lx0, 16)
-    sy.dma_start(T.xs[:, 1024:2048], T.x[:, 1024:2048]).then_inc(S.lx1, 16)
-    sy.wait_ge(S.lx0, 16)
-    sy.dma_start(T.es[:], T.e[:]).then_inc(S.le, 16)
-    sy.dma_start(T.w2s[:], T.w2[:]).then_inc(S.lw2, 16)
+    for q, steps in ((se, SCALAR), (ve, VECTOR)):
+        for step in steps:
+            if step == "w1":
+                q.wait_ge(S.lw1, 16)
+                r = q.quantize_mx(T.w1q[:, 0:256], T.w1p[:, 0:256], T.w1s[:, 0:1024])
+            elif step == "w2":
+                q.wait_ge(S.lw2, 16)
+                r = q.quantize_mx(T.w2q[:, 0:128], T.w2p[:, 0:128], T.w2s[:, 0:512])
+            elif step == "e":
+                q.wait_ge(S.le, 16)
+                r = q.quantize_mx(T.eq[:, 0:256], T.ep[:, 0:256], T.es[:, 0:1024])
+            elif step[0] == "x":
+                a, b = XQ[int(step[1])]
+                for i in over(XL, a, b):
+                    q.wait_ge(S["lx%d" % i], 16)
+                r = q.quantize_mx(T.xq[:, a:b], T.xp[:, a:b], T.xs[:, 4 * a:4 * b])
+            elif step[0] == "H":
+                p = int(step[1])
+                a, b = HP[p]
+                need(q, *h_acts(p))
+                r = q.quantize_mx(T.hq[:, a:b], T.hp[:, a:b], T.ht[:, 4 * a:4 * b])
+            elif step[0] == "K":
+                s = int(step[1])
+                a, b = KP[s]
+                need(q, *["ak%d%d" % (t, s) for t in range(4)])
+                r = q.quantize_mx(T.kq[:, a:b], T.kp[:, a:b], T.kt[:, 4 * a:4 * b])
+            elif step[0] == "h":
+                p, i, s = int(step[1]), int(step[2]), int(step[3])
+                a, b = HP[p]
+                c = 512 * ((2 * p + i) % 4)
+                need(q, "mh%d%d" % (p, i))
+                turn(q, steps, step)
+                r = part(q, T.ht[:, 4 * a + 2 * i + s:4 * b:4], T.pz[:, c:c + b - a], signs[s])
+            elif step[0] == "k":
+                t, s = int(step[1]), int(step[2])
+                a, b = KP[s]
+                need(q, "mk%d" % t)
+                turn(q, steps, step)
+                r = part(q, T.kt[:, 4 * a + t:4 * b:4], T.pk[:, 512 * t:512 * t + 256], signs[s])
+            elif step[0] == "z":
+                b = int(step[1])
+                need(q, "mz%d" % b)
+                r = out_of(q, T.zo[:, 256 * b:256 * b + 256], T.pk[:, 512 * b:512 * b + 256])
+            else:
+                j = int(step[1])
+                a, b = YP[j]
+                need(q, "my%d" % j)
+                r = out_of(q, T.yo[:, a:b], T.pz[:, 512 * j:512 * j + b - a])
+            r.then_inc(S["a" + step], 1)
 
-    def plain(half):
-        for i in range(2):
-            b = 1024 * half + 512 * i
-            te.matmul_mx(T.pz[:, b:b + 256], T.w1q[:, 128 * i:128 * i + 128], T.w1p[:, 128 * i:128 * i + 128],
-                         T.xq[:, 256 * half:256 * half + 256], T.xp[:, 256 * half:256 * half + 256],
-                         True, True).then_inc(S["mh%d" % (2 * half + i)], 1)
-
-    def turned(t):
-        te.matmul_mx(T.pk[:, 512 * t:512 * t + 256], T.xq[:, 128 * t:128 * t + 128], T.xp[:, 128 * t:128 * t + 128],
-                     T.w1q[:, 0:256], T.w1p[:, 0:256], True, True).then_inc(S["mk%d" % t], 1)
-
-    te.wait_ge(S.qw1, 1)
-    te.wait_ge(S.qx0, 1)
-    plain(0)
-    turned(0)
-    turned(1)
-    te.wait_ge(S.qx1, 1)
-    turned(2)
-    turned(3)
-    plain(1)
-    te.wait_ge(S.qe, 1)
-    te.wait_ge(S.aks, 6)
-    te.wait_ge(S.akv, 2)
-    te.wait_ge(S.rk, 2 * engines(topo, behind, core))
-    for b in range(4):
-        c = 128 * ORDER.index(b)
-        te.matmul_mx(T.pk[:, 512 * b:512 * b + 256], T.rkq[:, c:c + 128], T.rkp[:, c:c + 128],
-                     T.eq[:, 0:256], T.ep[:, 0:256], True, True).then_inc(S["mz%d" % b], 1)
-    te.wait_ge(S.qw2, 1)
-    for s in ("ahs0", "ahv0", "ahs1", "ahv1"):
-        te.wait_ge(S[s], 2)
-    for s in ("rh0", "rhp"):
-        te.wait_ge(S[s], engines(topo, before, core))
-    for i, (c, w) in enumerate(YCUT):
-        if i == 1:
-            te.wait_ge(S.rh1, engines(topo, before, core))
-        te.matmul_mx(T.pz[:, 512 * i:512 * i + w], T.w2q[:, 0:128], T.w2p[:, 0:128],
-                     T.rhq[:, c:c + w], T.rhp[:, c:c + w], True, True).then_inc(S["my%d" % i], 1)
-
-    def z_out(q, b):
-        q.wait_ge(S["mz%d" % b], 1)
-        o, i = T.zo[:, 256 * b:256 * b + 256], T.pk[:, 512 * b:512 * b + 256]
-        (se.activation(o, i, copy) if q is se else ve.tensor_copy(o, i)).then_inc(S["ez%d" % b], 1)
-
-    def y_out(q, j):
-        c, w = YCUT[j]
-        q.wait_ge(S["my%d" % j], 1)
-        o, i = T.yo[:, c:c + w], T.pz[:, 512 * j:512 * j + w]
-        (se.activation(o, i, copy) if q is se else ve.tensor_copy(o, i)).then_inc(S["ey%d" % j], 1)
-
-    h_parts(se, 0, 0, S.ahs0)
-    for t in range(3):
-        k_parts(se, t, S.aks)
-    h_parts(se, 1, 0, S.ahs1)
-    z_out(se, 0)
-    z_out(se, 2)
-    y_out(se, 0)
-    y_out(se, 1)
-    se.wait_ge(S.ey1, 1)
-    se.wait_ge(S.ey2, 1)
-    se.dma_start(T.y[:, 256:512], T.yo[:, 256:512]).then_inc(S.stya, 16)
-    se.wait_ge(S.stya, 16)
-
-    ve.wait_ge(S.lw1, 16)
-    ve.quantize_mx(T.w1q[:, 0:256], T.w1p[:, 0:256], T.w1s[:, 0:1024]).then_inc(S.qw1, 1)
-    ve.wait_ge(S.lx0, 16)
-    ve.quantize_mx(T.xq[:, 0:256], T.xp[:, 0:256], T.xs[:, 0:1024]).then_inc(S.qx0, 1)
-    h_parts(ve, 0, 1, S.ahv0)
-    ve.wait_ge(S.lx1, 16)
-    ve.quantize_mx(T.xq[:, 256:512], T.xp[:, 256:512], T.xs[:, 1024:2048]).then_inc(S.qx1, 1)
-    ve.wait_ge(S.ahv0, 2)
-    ve.wait_ge(S.ahs0, 2)
-    ve.quantize_mx(T.hq[:, 0:256], T.hp[:, 0:256], T.ht[:, 0:1024]).then_inc(S.qh0, 1)
-    k_parts(ve, 3, S.akv)
-    ve.wait_ge(S.akv, 2)
-    ve.wait_ge(S.aks, 6)
-    ve.quantize_mx(T.kq[:, 0:512], T.kp[:, 0:512], T.kt[:, 0:2048]).then_inc(S.qk, 1)
-    h_parts(ve, 1, 1, S.ahv1)
-    ve.wait_ge(S.ahv1, 2)
-    ve.wait_ge(S.ahs1, 2)
-    ve.quantize_mx(T.hq[:, 256:512], T.hp[:, 256:512], T.ht[:, 1024:2048]).then_inc(S.qh1, 1)
-    ve.wait_ge(S.le, 16)
-    ve.quantize_mx(T.eq[:, 0:256], T.ep[:, 0:256], T.es[:, 0:1024]).then_inc(S.qe, 1)
-    ve.wait_ge(S.lw2, 16)
-    ve.quantize_mx(T.w2q[:, 0:128], T.w2p[:, 0:128], T.w2s[:, 0:512]).then_inc(S.qw2, 1)
-    z_out(ve, 1)
-    z_out(ve, 3)
-    y_out(ve, 2)
-
-    def codes(dst, land, src, a, b, arrive):
+    for step in SENDS:
+        dst = before if step[0] == "k" else behind
         rid, pid = topo.addr(dst, core)
-        g.remote_dma(land[:, a:b].bitcast(dt.uint8), src[:, a:b].bitcast(dt.uint8), arrive, S.sent, pid, rid, topo.mask(core, dst))
+        m = topo.mask(core, dst)
+        if step == "kp":
+            need(g, "aK0", "aK1")
+            g.remote_dma(T.rkp[:, 0:512], T.kp[:, 0:512], S.rkp, S.sent, pid, rid, m)
+        elif step == "hp":
+            need(g, *["aH%d" % p for p in range(len(HP))])
+            g.remote_dma(T.rhp[:, 0:512], T.hp[:, 0:512], S.rhp, S.sent, pid, rid, m)
+        else:
+            need(g, "a" + step.upper())
+            a, b = (KP if step[0] == "k" else HP)[int(step[1])]
+            land, src = (T.rkq, T.kq) if step[0] == "k" else (T.rhq, T.hq)
+            g.remote_dma(land[:, a:b].bitcast(dt.uint8), src[:, a:b].bitcast(dt.uint8), S["r" + step], S.sent, pid, rid, m)
+    g.wait_ge(S.sent, (1 + len(KP)) * engines(topo, core, before) + (1 + len(HP)) * engines(topo, core, behind))
 
-    def plane(dst, land, src, arrive):
-        rid, pid = topo.addr(dst, core)
-        g.remote_dma(land[:, 0:512], src[:, 0:512], arrive, S.sent, pid, rid, topo.mask(core, dst))
-
-    g.wait_ge(S.qh0, 1)
-    codes(behind, T.rhq, T.hq, 0, 256, S.rh0)
-    g.wait_ge(S.qk, 1)
-    codes(before, T.rkq, T.kq, 0, 512, S.rk)
-    plane(before, T.rkp, T.kp, S.rk)
-    g.wait_ge(S.qh1, 1)
-    plane(behind, T.rhp, T.hp, S.rhp)
-    codes(behind, T.rhq, T.hq, 256, 512, S.rh1)
-    g.wait_ge(S.sent, 3 * engines(topo, core, behind) + 2 * engines(topo, core, before))
-
-    for b in range(4):
-        sy.wait_ge(S["ez%d" % b], 1)
-        if b % 2:
-            sy.dma_start(T.z[:, 256 * b - 256:256 * b + 256], T.zo[:, 256 * b - 256:256 * b + 256]).then_inc(S.stz, 16)
-    sy.wait_ge(S.ey0, 1)
-    sy.dma_start(T.y[:, 0:256], T.yo[:, 0:256]).then_inc(S.stys, 16)
-    sy.wait_ge(S.stz, 32)
-    sy.wait_ge(S.stys, 16)
+    for b in ORDER:
+        need(sy, "az%d" % b)
+        sy.dma_start(T.z[:, 256 * b:256 * b + 256], T.zo[:, 256 * b:256 * b + 256]).then_inc(S.stz, 16)
+    for i, ((a, b), pieces) in enumerate(YS):
+        q = se if i == len(YS) - 1 else sy
+        need(q, *["ay%d" % j for j in pieces])
+        q.dma_start(T.y[:, a:b], T.yo[:, a:b]).then_inc(S["sty%d" % i], 16)
+    sy.wait_ge(S.stz, 16 * 4)
+    for i in range(len(YS)):
+        sy.wait_ge(S["sty%d" % i], 16)

@@ -4,16 +4,25 @@ from concourse.mybir import dt, AluOpType, ActivationFunctionType
 CODE, PLANE, BF16, F32 = "float8_e4m3fn_x4", "uint8", "bfloat16", "float32"
 C = float(np.float32(0.047))
 ORDER = [0, 2, 1, 3]
+SAME_DIE = False
+E = 288
+WP = ((0, 128), (128, 256))
 XL = ((0, 128), (128, 512))
-XQ = ((0, 128), (128, 256), (256, 512))
-HP = ((0, 128), (128, 256), (256, 512))
+XQ = ((0, 128), (128, E), (E, 512))
+HP = ((0, 128), (128, E), (E, 512))
+HOWN = "hhr"
 KP = ((0, 256), (256, 512))
-YP = ((0, 256), (256, 384), (384, 512))
-YS = (((0, 256), (0,)), ((256, 512), (1, 2)))
-TENSOR = "h0 k0 h1 k1 k2 k3 h2".split()
-SCALAR = "h000 h001 k00 k01 h100 h101 k10 k20 k11 k21 h200 h201 z0 z1 y0 y1".split()
-VECTOR = "w1 x0 h010 h011 x1 H0 x2 h110 h111 H1 k30 K0 k31 K1 h210 h211 H2 e w2 z2 z3 y2".split()
-SENDS = "h0 h1 k0 kp k1 hp h2".split()
+YP = ((E, 512), (0, 128), (128, E))
+YS = (((E, 512), (0,)), ((0, E), (1, 2)))
+FREE = ("x1", "p1")
+TENSOR = "k0 k1 k2 k3 h2".split()
+SCALAR = "k00 k10 k01 k11 h200 h201 z0 z1 y0 y1".split()
+VECTOR = "w10 w11 x0 x1 x2 k20 k30 K0 k21 k31 K1 h210 h211 H2 e w2 z2 z3 y2".split()
+SENDS = "w0 w1 x0 wp p0 x1 p1 k0 kp k1 hp h2".split()
+HTENSOR = "h0 h1".split()
+HSCALAR = "h000 h001 h100 h101".split()
+HVECTOR = "h010 h011 H0 h110 h111 H1".split()
+HSENDS = "h0 hp h1".split()
 
 SCRATCH = {
     "xs": ("sbuf", [128, 2048], BF16), "w1s": ("sbuf", [128, 1024], BF16),
@@ -30,32 +39,56 @@ SCRATCH = {
     "yo": ("sbuf", [128, 512], F32), "zo": ("sbuf", [128, 1024], F32),
     "pk": ("psum", [128, 2048], F32), "pz": ("psum", [128, 2048], F32),
 }
-SEMAPHORES = (["lw1", "lw2", "le", "rkp", "rhp", "sent", "stz"] + ["lx%d" % i for i in range(len(XL))]
+SEMAPHORES = (["lw2", "le", "rkp", "rhp", "rhpr", "sent", "stz", "rwp"] + ["lx%d" % i for i in range(len(XL))]
+              + ["lw1%d" % i for i in range(len(WP))] + ["rw%d" % i for i in range(len(WP))]
+              + ["rx%d" % i for i in range(len(XQ))] + ["rp%d" % i for i in range(len(XQ))]
               + ["rh%d" % i for i in range(len(HP))] + ["rk%d" % i for i in range(len(KP))]
               + ["sty%d" % i for i in range(len(YS))]
               + ["mk%d" % t for t in range(4)] + ["mh%d%d" % (p, i) for p in range(len(HP)) for i in range(2)]
               + ["mz%d" % b for b in range(4)] + ["my%d" % j for j in range(len(YP))]
-              + ["a" + s for s in SCALAR] + ["a" + s for s in VECTOR])
-
-
-def engines(topo, src, dst):
-    return bin(topo.mask(src, dst)).count("1")
+              + ["a" + s for s in SCALAR + VECTOR + HSCALAR + HVECTOR])
 
 
 def over(pieces, a, b):
     return [i for i, (c, d) in enumerate(pieces) if c < b and a < d]
 
 
+def owned(who):
+    return [i for i in range(len(HP)) if HOWN[i] == who]
+
+
+def span(who):
+    return HP[owned(who)[0]][0], HP[owned(who)[-1]][1]
+
+
+def helper(topo, cores, c):
+    for d in range(256):
+        if (d not in cores and topo.host(d) == topo.host(c) and topo.chip(d) == topo.chip(c)
+                and (topo.die(d) == topo.die(c)) == SAME_DIE):
+            return d
+
+
 def rank_program(g, core, T, topo):
-    rank = T.rank_of(core)
-    if rank is None:
-        return
     n = len(T.cores)
+    helpers = [helper(topo, T.cores, c) for c in T.cores]
+    is_rank = T.rank_of(core) is not None
+    if not is_rank and core not in helpers:
+        return
+    rank = T.rank_of(core) if is_rank else helpers.index(core)
+    owner, aide = T.cores[rank], helpers[rank]
+    before, behind = T.cores[(rank - 1) % n], T.cores[(rank + 1) % n]
+    aide_before = helpers[(rank - 1) % n]
     S = T.sem
     te, ve, se, sy = g.tensor, g.vector, g.scalar, g.sync
     relu, copy = ActivationFunctionType.Relu, ActivationFunctionType.Copy
-    before, behind = T.cores[(rank - 1) % n], T.cores[(rank + 1) % n]
     signs = (1.0, -1.0)
+
+    def mask(step, src, dst):
+        m = topo.mask(src, dst)
+        return m & ~topo.mask(owner, behind) if step in FREE else m
+
+    def engines(step, src, dst):
+        return bin(mask(step, src, dst)).count("1")
 
     def need(q, *names):
         for s in names:
@@ -64,45 +97,65 @@ def rank_program(g, core, T, topo):
     def h_acts(p):
         return ["ah%d%d%d" % (p, i, s) for i in range(2) for s in range(2)]
 
-    se.dma_start(T.w1s[:], T.w1[:]).then_inc(S.lw1, 16)
-    for i, (a, b) in enumerate(XL):
-        sy.dma_start(T.xs[:, 4 * a:4 * b], T.x[:, 4 * a:4 * b]).then_inc(S["lx%d" % i], 16)
-    sy.wait_ge(S.lx0, 16)
-    sy.dma_start(T.es[:], T.e[:]).then_inc(S.le, 16)
-    sy.dma_start(T.w2s[:], T.w2[:]).then_inc(S.lw2, 16)
+    def bank(p, i):
+        return 512 * (2 * owned(HOWN[p]).index(p) + i)
 
-    need(te, "aw1")
-    for step in TENSOR:
+    def have_w1(q):
+        if is_rank:
+            need(q, *["aw1%d" % i for i in range(len(WP))])
+        else:
+            for s in ["w%d" % i for i in range(len(WP))] + ["wp"]:
+                q.wait_ge(S["r" + s], engines(s, owner, aide))
+
+    def have_x(q, a, b):
+        for i in over(XQ, a, b):
+            if is_rank:
+                need(q, "ax%d" % i)
+            else:
+                for s in ("x%d" % i, "p%d" % i):
+                    q.wait_ge(S["r" + s], engines(s, owner, aide))
+
+    if is_rank:
+        for i, (a, b) in enumerate(WP):
+            se.dma_start(T.w1s[:, 4 * a:4 * b], T.w1[:, 4 * a:4 * b]).then_inc(S["lw1%d" % i], 16)
+        for i, (a, b) in enumerate(XL):
+            sy.dma_start(T.xs[:, 4 * a:4 * b], T.x[:, 4 * a:4 * b]).then_inc(S["lx%d" % i], 16)
+        sy.wait_ge(S.lx0, 16)
+        sy.dma_start(T.es[:], T.e[:]).then_inc(S.le, 16)
+        sy.dma_start(T.w2s[:], T.w2[:]).then_inc(S.lw2, 16)
+
+    have_w1(te)
+    for step in TENSOR if is_rank else HTENSOR:
         j = int(step[1])
         if step[0] == "h":
             a, b = HP[j]
-            need(te, *["ax%d" % i for i in over(XQ, a, b)])
-            if j > 1:
-                need(te, *h_acts(j - 2))
+            have_x(te, a, b)
             for i in range(2):
-                c = 512 * ((2 * j + i) % 4)
+                c = bank(j, i)
                 te.matmul_mx(T.pz[:, c:c + b - a], T.w1q[:, 128 * i:128 * i + 128], T.w1p[:, 128 * i:128 * i + 128],
                              T.xq[:, a:b], T.xp[:, a:b], True, True).then_inc(S["mh%d%d" % (j, i)], 1)
         else:
             a, b = 128 * j, 128 * j + 128
-            need(te, *["ax%d" % i for i in over(XQ, a, b)])
+            have_x(te, a, b)
             te.matmul_mx(T.pk[:, 512 * j:512 * j + 256], T.xq[:, a:b], T.xp[:, a:b],
                          T.w1q[:, 0:256], T.w1p[:, 0:256], True, True).then_inc(S["mk%d" % j], 1)
-    need(te, "ae", *["ak%d%d" % (t, s) for t in range(4) for s in range(2)])
-    te.wait_ge(S.rkp, engines(topo, behind, core))
-    for b in ORDER:
-        c = 128 * ORDER.index(b)
-        for i in over(KP, c, c + 128):
-            te.wait_ge(S["rk%d" % i], engines(topo, behind, core))
-        te.matmul_mx(T.pk[:, 512 * b:512 * b + 256], T.rkq[:, c:c + 128], T.rkp[:, c:c + 128],
-                     T.eq[:, 0:256], T.ep[:, 0:256], True, True).then_inc(S["mz%d" % b], 1)
-    need(te, "aw2", *[s for p in range(len(HP)) for s in h_acts(p)])
-    te.wait_ge(S.rhp, engines(topo, before, core))
-    for j, (a, b) in enumerate(YP):
-        for i in over(HP, a, b):
-            te.wait_ge(S["rh%d" % i], engines(topo, before, core))
-        te.matmul_mx(T.pz[:, 512 * j:512 * j + b - a], T.w2q[:, 0:128], T.w2p[:, 0:128],
-                     T.rhq[:, a:b], T.rhp[:, a:b], True, True).then_inc(S["my%d" % j], 1)
+    if is_rank:
+        need(te, "ae", *["ak%d%d" % (t, s) for t in range(4) for s in range(2)])
+        te.wait_ge(S.rkp, engines("kp", behind, core))
+        for b in ORDER:
+            c = 128 * ORDER.index(b)
+            for i in over(KP, c, c + 128):
+                te.wait_ge(S["rk%d" % i], engines("k%d" % i, behind, core))
+            te.matmul_mx(T.pk[:, 512 * b:512 * b + 256], T.rkq[:, c:c + 128], T.rkp[:, c:c + 128],
+                         T.eq[:, 0:256], T.ep[:, 0:256], True, True).then_inc(S["mz%d" % b], 1)
+        need(te, "aw2", *[s for p in owned("r") for s in h_acts(p)])
+        for j, (a, b) in enumerate(YP):
+            for i in over(HP, a, b):
+                src, plane = (aide_before, "rhp") if HOWN[i] == "h" else (before, "rhpr")
+                te.wait_ge(S[plane], engines("hp", src, core))
+                te.wait_ge(S["rh%d" % i], engines("h%d" % i, src, core))
+            te.matmul_mx(T.pz[:, 512 * j:512 * j + b - a], T.w2q[:, 0:128], T.w2p[:, 0:128],
+                         T.rhq[:, a:b], T.rhp[:, a:b], True, True).then_inc(S["my%d" % j], 1)
 
     def part(q, out, src, sign):
         if q is se:
@@ -117,11 +170,13 @@ def rank_program(g, core, T, topo):
         if step[-1] == "1" and first not in mine:
             need(q, "a" + first)
 
-    for q, steps in ((se, SCALAR), (ve, VECTOR)):
+    for q, steps in ((se, SCALAR), (ve, VECTOR)) if is_rank else ((se, HSCALAR), (ve, HVECTOR)):
         for step in steps:
-            if step == "w1":
-                q.wait_ge(S.lw1, 16)
-                r = q.quantize_mx(T.w1q[:, 0:256], T.w1p[:, 0:256], T.w1s[:, 0:1024])
+            if step[:2] == "w1":
+                i = int(step[2])
+                a, b = WP[i]
+                q.wait_ge(S["lw1%d" % i], 16)
+                r = q.quantize_mx(T.w1q[:, a:b], T.w1p[:, a:b], T.w1s[:, 4 * a:4 * b])
             elif step == "w2":
                 q.wait_ge(S.lw2, 16)
                 r = q.quantize_mx(T.w2q[:, 0:128], T.w2p[:, 0:128], T.w2s[:, 0:512])
@@ -146,7 +201,7 @@ def rank_program(g, core, T, topo):
             elif step[0] == "h":
                 p, i, s = int(step[1]), int(step[2]), int(step[3])
                 a, b = HP[p]
-                c = 512 * ((2 * p + i) % 4)
+                c = bank(p, i)
                 need(q, "mh%d%d" % (p, i))
                 turn(q, steps, step)
                 r = part(q, T.ht[:, 4 * a + 2 * i + s:4 * b:4], T.pz[:, c:c + b - a], signs[s])
@@ -167,30 +222,45 @@ def rank_program(g, core, T, topo):
                 r = out_of(q, T.yo[:, a:b], T.pz[:, 512 * j:512 * j + b - a])
             r.then_inc(S["a" + step], 1)
 
-    for step in SENDS:
-        dst = before if step[0] == "k" else behind
-        rid, pid = topo.addr(dst, core)
-        m = topo.mask(core, dst)
+    def write(step):
+        kind, i = step[0], step[1]
         if step == "kp":
-            need(g, "aK0", "aK1")
-            g.remote_dma(T.rkp[:, 0:512], T.kp[:, 0:512], S.rkp, S.sent, pid, rid, m)
-        elif step == "hp":
-            need(g, *["aH%d" % p for p in range(len(HP))])
-            g.remote_dma(T.rhp[:, 0:512], T.hp[:, 0:512], S.rhp, S.sent, pid, rid, m)
-        else:
-            need(g, "a" + step.upper())
-            a, b = (KP if step[0] == "k" else HP)[int(step[1])]
-            land, src = (T.rkq, T.kq) if step[0] == "k" else (T.rhq, T.hq)
-            g.remote_dma(land[:, a:b].bitcast(dt.uint8), src[:, a:b].bitcast(dt.uint8), S["r" + step], S.sent, pid, rid, m)
-    g.wait_ge(S.sent, (1 + len(KP)) * engines(topo, core, before) + (1 + len(HP)) * engines(topo, core, behind))
+            need(g, *["aK%d" % j for j in range(len(KP))])
+            return T.rkp[:, 0:512], T.kp[:, 0:512], S.rkp
+        if step == "hp":
+            own = "r" if is_rank else "h"
+            need(g, *["aH%d" % p for p in owned(own)])
+            a, b = span(own)
+            return T.rhp[:, a:b], T.hp[:, a:b], S["rhpr" if is_rank else "rhp"]
+        if step == "wp":
+            have_w1(g)
+            return T.w1p[:, 0:256], T.w1p[:, 0:256], S.rwp
+        if kind == "p":
+            need(g, "ax" + i)
+            a, b = XQ[int(i)]
+            return T.xp[:, a:b], T.xp[:, a:b], S["rp" + i]
+        need(g, {"w": "aw1", "x": "ax", "k": "aK", "h": "aH"}[kind] + i)
+        a, b = {"w": WP, "x": XQ, "k": KP, "h": HP}[kind][int(i)]
+        land, src = {"w": (T.w1q, T.w1q), "x": (T.xq, T.xq), "k": (T.rkq, T.kq), "h": (T.rhq, T.hq)}[kind]
+        return land[:, a:b].bitcast(dt.uint8), src[:, a:b].bitcast(dt.uint8), S["r" + step]
 
-    for b in ORDER:
-        need(sy, "az%d" % b)
-        sy.dma_start(T.z[:, 256 * b:256 * b + 256], T.zo[:, 256 * b:256 * b + 256]).then_inc(S.stz, 16)
-    for i, ((a, b), pieces) in enumerate(YS):
-        q = se if i == len(YS) - 1 else sy
-        need(q, *["ay%d" % j for j in pieces])
-        q.dma_start(T.y[:, a:b], T.yo[:, a:b]).then_inc(S["sty%d" % i], 16)
-    sy.wait_ge(S.stz, 16 * 4)
-    for i in range(len(YS)):
-        sy.wait_ge(S["sty%d" % i], 16)
+    total = 0
+    for step in SENDS if is_rank else HSENDS:
+        dst = before if step[0] == "k" else behind if step[0] == "h" else aide
+        rid, pid = topo.addr(dst, core)
+        out, in_, landed = write(step)
+        g.remote_dma(out, in_, landed, S.sent, pid, rid, mask(step, core, dst))
+        total += engines(step, core, dst)
+    g.wait_ge(S.sent, total)
+
+    if is_rank:
+        for b in ORDER:
+            need(sy, "az%d" % b)
+            sy.dma_start(T.z[:, 256 * b:256 * b + 256], T.zo[:, 256 * b:256 * b + 256]).then_inc(S.stz, 16)
+        for i, ((a, b), pieces) in enumerate(YS):
+            q = se if i == len(YS) - 1 else sy
+            need(q, *["ay%d" % j for j in pieces])
+            q.dma_start(T.y[:, a:b], T.yo[:, a:b]).then_inc(S["sty%d" % i], 16)
+        sy.wait_ge(S.stz, 16 * 4)
+        for i in range(len(YS)):
+            sy.wait_ge(S["sty%d" % i], 16)

import numpy as np
from concourse.mybir import dt, AluOpType, ActivationFunctionType

CODE, PLANE, BF16, F32 = "float8_e4m3fn_x4", "uint8", "bfloat16", "float32"
C = float(np.float32(0.047))
ORDER = [0, 2, 1, 3]
SAME_DIE = False
E = 288
WP = ((0, 128), (128, 256))
XL = ((0, 128), (128, 512))
XQ = ((0, 128), (128, E), (E, 512))
HP = ((0, 128), (128, E), (E, 512))
HOWN = "hhr"
KP = ((0, 256), (256, 512))
YP = ((E, 512), (0, 128), (128, E))
YS = (((E, 512), (0,)), ((0, E), (1, 2)))
FREE = ("x1", "p1")
TENSOR = "k0 k1 k2 k3 h2".split()
SCALAR = "k00 k10 k01 k11 h200 h201 z0 z1 y0 y1".split()
VECTOR = "w10 w11 x0 x1 x2 k20 k30 K0 k21 k31 K1 h210 h211 H2 e w2 z2 z3 y2".split()
SENDS = "w0 w1 x0 wp p0 x1 p1 k0 kp k1 hp h2".split()
HTENSOR = "h0 h1".split()
HSCALAR = "h000 h001 h100 h101".split()
HVECTOR = "h010 h011 H0 h110 h111 H1".split()
HSENDS = "h0 hp h1".split()

SCRATCH = {
    "xs": ("sbuf", [128, 2048], BF16), "w1s": ("sbuf", [128, 1024], BF16),
    "w2s": ("sbuf", [128, 512], BF16), "es": ("sbuf", [128, 1024], BF16),
    "xq": ("sbuf", [128, 512], CODE), "xp": ("sbuf", [128, 512], PLANE),
    "w1q": ("sbuf", [128, 256], CODE), "w1p": ("sbuf", [128, 256], PLANE),
    "w2q": ("sbuf", [128, 128], CODE), "w2p": ("sbuf", [128, 128], PLANE),
    "eq": ("sbuf", [128, 256], CODE), "ep": ("sbuf", [128, 256], PLANE),
    "ht": ("sbuf", [128, 2048], BF16), "kt": ("sbuf", [128, 2048], BF16),
    "hq": ("sbuf", [128, 512], CODE), "hp": ("sbuf", [128, 512], PLANE),
    "kq": ("sbuf", [128, 512], CODE), "kp": ("sbuf", [128, 512], PLANE),
    "rhq": ("sbuf", [128, 512], CODE), "rhp": ("sbuf", [128, 512], PLANE),
    "rkq": ("sbuf", [128, 512], CODE), "rkp": ("sbuf", [128, 512], PLANE),
    "yo": ("sbuf", [128, 512], F32), "zo": ("sbuf", [128, 1024], F32),
    "pk": ("psum", [128, 2048], F32), "pz": ("psum", [128, 2048], F32),
}
SEMAPHORES = (["lw2", "le", "rkp", "rhp", "rhpr", "sent", "stz", "rwp"] + ["lx%d" % i for i in range(len(XL))]
              + ["lw1%d" % i for i in range(len(WP))] + ["rw%d" % i for i in range(len(WP))]
              + ["rx%d" % i for i in range(len(XQ))] + ["rp%d" % i for i in range(len(XQ))]
              + ["rh%d" % i for i in range(len(HP))] + ["rk%d" % i for i in range(len(KP))]
              + ["sty%d" % i for i in range(len(YS))]
              + ["mk%d" % t for t in range(4)] + ["mh%d%d" % (p, i) for p in range(len(HP)) for i in range(2)]
              + ["mz%d" % b for b in range(4)] + ["my%d" % j for j in range(len(YP))]
              + ["a" + s for s in SCALAR + VECTOR + HSCALAR + HVECTOR])


def over(pieces, a, b):
    return [i for i, (c, d) in enumerate(pieces) if c < b and a < d]


def owned(who):
    return [i for i in range(len(HP)) if HOWN[i] == who]


def span(who):
    return HP[owned(who)[0]][0], HP[owned(who)[-1]][1]


def helper(topo, cores, c):
    for d in range(256):
        if (d not in cores and topo.host(d) == topo.host(c) and topo.chip(d) == topo.chip(c)
                and (topo.die(d) == topo.die(c)) == SAME_DIE):
            return d


def rank_program(g, core, T, topo):
    n = len(T.cores)
    helpers = [helper(topo, T.cores, c) for c in T.cores]
    is_rank = T.rank_of(core) is not None
    if not is_rank and core not in helpers:
        return
    rank = T.rank_of(core) if is_rank else helpers.index(core)
    owner, aide = T.cores[rank], helpers[rank]
    before, behind = T.cores[(rank - 1) % n], T.cores[(rank + 1) % n]
    aide_before = helpers[(rank - 1) % n]
    S = T.sem
    te, ve, se, sy = g.tensor, g.vector, g.scalar, g.sync
    relu, copy = ActivationFunctionType.Relu, ActivationFunctionType.Copy
    signs = (1.0, -1.0)

    def mask(step, src, dst):
        m = topo.mask(src, dst)
        return m & ~topo.mask(owner, behind) if step in FREE else m

    def engines(step, src, dst):
        return bin(mask(step, src, dst)).count("1")

    def need(q, *names):
        for s in names:
            q.wait_ge(S[s], 1)

    def h_acts(p):
        return ["ah%d%d%d" % (p, i, s) for i in range(2) for s in range(2)]

    def bank(p, i):
        return 512 * (2 * owned(HOWN[p]).index(p) + i)

    def have_w1(q):
        if is_rank:
            need(q, *["aw1%d" % i for i in range(len(WP))])
        else:
            for s in ["w%d" % i for i in range(len(WP))] + ["wp"]:
                q.wait_ge(S["r" + s], engines(s, owner, aide))

    def have_x(q, a, b):
        for i in over(XQ, a, b):
            if is_rank:
                need(q, "ax%d" % i)
            else:
                for s in ("x%d" % i, "p%d" % i):
                    q.wait_ge(S["r" + s], engines(s, owner, aide))

    if is_rank:
        for i, (a, b) in enumerate(WP):
            se.dma_start(T.w1s[:, 4 * a:4 * b], T.w1[:, 4 * a:4 * b]).then_inc(S["lw1%d" % i], 16)
        for i, (a, b) in enumerate(XL):
            sy.dma_start(T.xs[:, 4 * a:4 * b], T.x[:, 4 * a:4 * b]).then_inc(S["lx%d" % i], 16)
        sy.wait_ge(S.lx0, 16)
        sy.dma_start(T.es[:], T.e[:]).then_inc(S.le, 16)
        sy.dma_start(T.w2s[:], T.w2[:]).then_inc(S.lw2, 16)

    have_w1(te)
    for step in TENSOR if is_rank else HTENSOR:
        j = int(step[1])
        if step[0] == "h":
            a, b = HP[j]
            have_x(te, a, b)
            for i in range(2):
                c = bank(j, i)
                te.matmul_mx(T.pz[:, c:c + b - a], T.w1q[:, 128 * i:128 * i + 128], T.w1p[:, 128 * i:128 * i + 128],
                             T.xq[:, a:b], T.xp[:, a:b], True, True).then_inc(S["mh%d%d" % (j, i)], 1)
        else:
            a, b = 128 * j, 128 * j + 128
            have_x(te, a, b)
            te.matmul_mx(T.pk[:, 512 * j:512 * j + 256], T.xq[:, a:b], T.xp[:, a:b],
                         T.w1q[:, 0:256], T.w1p[:, 0:256], True, True).then_inc(S["mk%d" % j], 1)
    if is_rank:
        need(te, "ae", *["ak%d%d" % (t, s) for t in range(4) for s in range(2)])
        te.wait_ge(S.rkp, engines("kp", behind, core))
        for b in ORDER:
            c = 128 * ORDER.index(b)
            for i in over(KP, c, c + 128):
                te.wait_ge(S["rk%d" % i], engines("k%d" % i, behind, core))
            te.matmul_mx(T.pk[:, 512 * b:512 * b + 256], T.rkq[:, c:c + 128], T.rkp[:, c:c + 128],
                         T.eq[:, 0:256], T.ep[:, 0:256], True, True).then_inc(S["mz%d" % b], 1)
        need(te, "aw2", *[s for p in owned("r") for s in h_acts(p)])
        for j, (a, b) in enumerate(YP):
            for i in over(HP, a, b):
                src, plane = (aide_before, "rhp") if HOWN[i] == "h" else (before, "rhpr")
                te.wait_ge(S[plane], engines("hp", src, core))
                te.wait_ge(S["rh%d" % i], engines("h%d" % i, src, core))
            te.matmul_mx(T.pz[:, 512 * j:512 * j + b - a], T.w2q[:, 0:128], T.w2p[:, 0:128],
                         T.rhq[:, a:b], T.rhp[:, a:b], True, True).then_inc(S["my%d" % j], 1)

    def part(q, out, src, sign):
        if q is se:
            return se.activation(out, src, relu, scale=sign * C)
        return ve.tensor_scalar(out, src, sign * C, 0.0, AluOpType.mult, AluOpType.max)

    def out_of(q, out, src):
        return se.activation(out, src, copy) if q is se else ve.tensor_copy(out, src)

    def turn(q, mine, step):
        first = step[:-1] + "0"
        if step[-1] == "1" and first not in mine:
            need(q, "a" + first)

    for q, steps in ((se, SCALAR), (ve, VECTOR)) if is_rank else ((se, HSCALAR), (ve, HVECTOR)):
        for step in steps:
            if step[:2] == "w1":
                i = int(step[2])
                a, b = WP[i]
                q.wait_ge(S["lw1%d" % i], 16)
                r = q.quantize_mx(T.w1q[:, a:b], T.w1p[:, a:b], T.w1s[:, 4 * a:4 * b])
            elif step == "w2":
                q.wait_ge(S.lw2, 16)
                r = q.quantize_mx(T.w2q[:, 0:128], T.w2p[:, 0:128], T.w2s[:, 0:512])
            elif step == "e":
                q.wait_ge(S.le, 16)
                r = q.quantize_mx(T.eq[:, 0:256], T.ep[:, 0:256], T.es[:, 0:1024])
            elif step[0] == "x":
                a, b = XQ[int(step[1])]
                for i in over(XL, a, b):
                    q.wait_ge(S["lx%d" % i], 16)
                r = q.quantize_mx(T.xq[:, a:b], T.xp[:, a:b], T.xs[:, 4 * a:4 * b])
            elif step[0] == "H":
                p = int(step[1])
                a, b = HP[p]
                need(q, *h_acts(p))
                r = q.quantize_mx(T.hq[:, a:b], T.hp[:, a:b], T.ht[:, 4 * a:4 * b])
            elif step[0] == "K":
                s = int(step[1])
                a, b = KP[s]
                need(q, *["ak%d%d" % (t, s) for t in range(4)])
                r = q.quantize_mx(T.kq[:, a:b], T.kp[:, a:b], T.kt[:, 4 * a:4 * b])
            elif step[0] == "h":
                p, i, s = int(step[1]), int(step[2]), int(step[3])
                a, b = HP[p]
                c = bank(p, i)
                need(q, "mh%d%d" % (p, i))
                turn(q, steps, step)
                r = part(q, T.ht[:, 4 * a + 2 * i + s:4 * b:4], T.pz[:, c:c + b - a], signs[s])
            elif step[0] == "k":
                t, s = int(step[1]), int(step[2])
                a, b = KP[s]
                need(q, "mk%d" % t)
                turn(q, steps, step)
                r = part(q, T.kt[:, 4 * a + t:4 * b:4], T.pk[:, 512 * t:512 * t + 256], signs[s])
            elif step[0] == "z":
                b = int(step[1])
                need(q, "mz%d" % b)
                r = out_of(q, T.zo[:, 256 * b:256 * b + 256], T.pk[:, 512 * b:512 * b + 256])
            else:
                j = int(step[1])
                a, b = YP[j]
                need(q, "my%d" % j)
                r = out_of(q, T.yo[:, a:b], T.pz[:, 512 * j:512 * j + b - a])
            r.then_inc(S["a" + step], 1)

    def write(step):
        kind, i = step[0], step[1]
        if step == "kp":
            need(g, *["aK%d" % j for j in range(len(KP))])
            return T.rkp[:, 0:512], T.kp[:, 0:512], S.rkp
        if step == "hp":
            own = "r" if is_rank else "h"
            need(g, *["aH%d" % p for p in owned(own)])
            a, b = span(own)
            return T.rhp[:, a:b], T.hp[:, a:b], S["rhpr" if is_rank else "rhp"]
        if step == "wp":
            have_w1(g)
            return T.w1p[:, 0:256], T.w1p[:, 0:256], S.rwp
        if kind == "p":
            need(g, "ax" + i)
            a, b = XQ[int(i)]
            return T.xp[:, a:b], T.xp[:, a:b], S["rp" + i]
        need(g, {"w": "aw1", "x": "ax", "k": "aK", "h": "aH"}[kind] + i)
        a, b = {"w": WP, "x": XQ, "k": KP, "h": HP}[kind][int(i)]
        land, src = {"w": (T.w1q, T.w1q), "x": (T.xq, T.xq), "k": (T.rkq, T.kq), "h": (T.rhq, T.hq)}[kind]
        return land[:, a:b].bitcast(dt.uint8), src[:, a:b].bitcast(dt.uint8), S["r" + step]

    total = 0
    for step in SENDS if is_rank else HSENDS:
        dst = before if step[0] == "k" else behind if step[0] == "h" else aide
        rid, pid = topo.addr(dst, core)
        out, in_, landed = write(step)
        g.remote_dma(out, in_, landed, S.sent, pid, rid, mask(step, core, dst))
        total += engines(step, core, dst)
    g.wait_ge(S.sent, total)

    if is_rank:
        for b in ORDER:
            need(sy, "az%d" % b)
            sy.dma_start(T.z[:, 256 * b:256 * b + 256], T.zo[:, 256 * b:256 * b + 256]).then_inc(S.stz, 16)
        for i, ((a, b), pieces) in enumerate(YS):
            q = se if i == len(YS) - 1 else sy
            need(q, *["ay%d" % j for j in pieces])
            q.dma_start(T.y[:, a:b], T.yo[:, a:b]).then_inc(S["sty%d" % i], 16)
        sy.wait_ge(S.stz, 16 * 4)
        for i in range(len(YS)):
            sy.wait_ge(S["sty%d" % i], 16)
